import numpy as np
import ml_dtypes


def mxq(x, axis, fmt="e4m3"):
    dtype, down = {"e4m3": (ml_dtypes.float8_e4m3fn, 7), "e5m2": (ml_dtypes.float8_e5m2, 14)}[fmt]
    v = np.moveaxis(np.asarray(x, np.float32).astype(ml_dtypes.bfloat16).astype(np.float64), axis, -1)
    blocks = v.reshape(v.shape[:-1] + (-1, 32))
    amax = np.abs(blocks).max(-1, keepdims=True)
    byte = np.maximum(np.where(amax > 0, np.frexp(amax)[1] - 1 + 127, 0) - down, 1)
    scale = np.exp2(byte - 127.0)
    codes = (blocks / scale).astype(np.float32).astype(dtype).astype(np.float64)
    return np.moveaxis((codes * scale).reshape(v.shape), -1, axis)


WIDE = False


def mx_kscale(k):
    if not WIDE:
        return np.ones(k)
    levels = np.array([10, -10, 5, -5, 0])
    if k % 512:
        return np.exp2(np.random.permutation(np.resize(levels, k // 32))).repeat(32)
    a = np.empty((k // 512, 16))
    for p in range(k // 512):
        a[p, :8] = np.random.permutation(np.resize(levels, 8))
        for g in range(8):
            far = levels[np.abs(levels - a[p, g]) >= 10]
            a[p, g + 8] = far[np.random.randint(len(far))]
    return np.exp2(a.ravel()).repeat(32)


BF16 = ml_dtypes.bfloat16


def bf(x):
    return np.asarray(x, np.float32).astype(BF16)


def f64(x):
    return np.asarray(x).astype(np.float64)


E2M1 = np.array([0.0, 0.5, 1.0, 1.5, 2.0, 3.0, 4.0, 6.0, -0.0, -0.5, -1.0, -1.5, -2.0, -3.0, -4.0, -6.0])


def pack_weight(w, fmt):
    k, n = w.shape
    w = f64(bf(w)).reshape(k // 32, 32, n)
    amax = np.abs(w).max(1)
    if fmt == "e4m3":
        byte = np.frexp(amax)[1] - 1 + 127 - 7
    else:
        mant, ex = np.frexp(amax / 6.0)
        byte = np.where(mant > 0.5, ex, ex - 1) + 127
    byte = np.clip(np.where(amax > 0, byte, 1), 1, 254)
    scaled = (w * np.exp2(127.0 - byte)[:, None, :]).reshape(k, n).astype(np.float32)
    by_word = np.ascontiguousarray(scaled.reshape(k // 512, 128, 4, n).transpose(0, 1, 3, 2))
    if fmt == "e4m3":
        words = by_word.astype(ml_dtypes.float8_e4m3fn).view(np.uint8)
    else:
        c = by_word.astype(ml_dtypes.float4_e2m1fn).view(np.uint8) & 0xF
        words = c[..., 0::2] | (c[..., 1::2] << 4)
    return np.ascontiguousarray(words), np.ascontiguousarray(byte.astype(np.uint8).reshape(k // 512, 16, n))


def unpack_weight(words, scales, fmt):
    g, p, n, _ = words.shape
    if fmt == "e4m3":
        vals = np.ascontiguousarray(words).view(ml_dtypes.float8_e4m3fn).astype(np.float64)
    else:
        nib = np.empty((g, p, n, 4), np.uint8)
        nib[..., 0::2] = words & 0xF
        nib[..., 1::2] = words >> 4
        vals = E2M1[nib]
    vals = vals * np.repeat(np.exp2(scales.astype(np.float64) - 127.0), 8, axis=1)[..., None]
    return vals.transpose(0, 1, 3, 2).reshape(g * 512, n)
def pack4(w):
    words, scales = pack_weight(w, "e2m1")
    return words.reshape(words.shape[0], 128, -1), scales


def unpack4(words, scales):
    return unpack_weight(words.reshape(words.shape[0], 128, -1, 2), scales, "e2m1")


E4M3FN = np.array([(-1.0 if i & 128 else 1.0) * ((1.0 + (i & 7) / 8.0) * 2.0 ** (((i >> 3) & 15) - 7) if i & 120 else (i & 7) * 2.0 ** -9) for i in range(256)])


def e4m3fn_bytes(y):
    return np.clip(np.asarray(y, np.float64), -448.0, 448.0).astype(np.float32).astype(ml_dtypes.float8_e4m3fn).view(np.uint8)


def e4m3fn_values(b):
    return E4M3FN[b]


T, K, J, D, B = 1024, 1024, 2048, 1024, 128


def setup_inputs():
    s, t = mx_kscale(K), mx_kscale(J)
    sigma = (0.5 / K) ** 0.25
    x = np.random.standard_normal((T, K)) * sigma
    c = np.random.standard_normal((J, K)) * sigma
    mean = K * sigma ** 2 / 2
    row = np.exp(mean - (x ** 2).sum(1) / 2)
    amp = np.exp(mean - (c ** 2).sum(1) / 2)
    x = x * s
    x_scale = (np.abs(x).reshape(T, K // B, B).max(2) / 448.0).astype(np.float32)
    w_words, w_scales = pack4(np.random.standard_normal((J, D)) / np.sqrt(J) / t[:, None])
    return {"X_bytes": e4m3fn_bytes(x / np.repeat(f64(x_scale), B, axis=1)),
            "X_scale": x_scale,
            "C": bf(c / s),
            "amp": bf(amp * t),
            "row": bf(row),
            "W_words": w_words,
            "W_scales": w_scales}


def reference(X_bytes, X_scale, C, amp, row, W_words, W_scales):
    x = e4m3fn_values(X_bytes) * np.repeat(f64(X_scale), B, axis=1)
    z = mxq(x, 1, "e4m3") @ mxq(f64(C), 1, "e4m3").T
    h = np.exp(z) * f64(amp)
    y = mxq(h, 1, "e4m3") @ unpack4(W_words, W_scales)
    return y * f64(row)[:, None]

@@ -1,0 +1,318 @@
+from contextlib import ExitStack
+
+import concourse.mybir as mybir
+from concourse.masks import make_identity
+
+T, K, J, D = 1024, 1024, 2048, 1024
+FLOPS = 2 * T * K * J + 2 * T * J * D
+
+F32 = mybir.dt.float32
+BF16 = mybir.dt.bfloat16
+U32 = mybir.dt.uint32
+I32 = mybir.dt.int32
+U8 = mybir.dt.uint8
+F8 = mybir.dt.float8_e4m3fn
+FP8X4 = mybir.dt.float8_e4m3fn_x4
+FP4X4 = mybir.dt.float4_e2m1fn_x4
+MULT = mybir.AluOpType.mult
+EXP = mybir.ActivationFunctionType.Exp
+COPY = mybir.ActivationFunctionType.Copy
+
+P = 128
+NT = T // P
+NQ = 4
+QT = T // NQ
+NG = J // 512
+
+
+def tile_rbf_kernel_readout_d4_kernel(tc, X_bytes, X_scale, C, amp, row, W_words, W_scales, out):
+    nc = tc.nc
+    with ExitStack() as ctx:
+        keep = ctx.enter_context(tc.tile_pool(name="keep", bufs=1))
+        stage = ctx.enter_context(tc.tile_pool(name="stage", bufs=3))
+        psum = ctx.enter_context(tc.psum_pool(name="psum", bufs=8))
+        ctx.enter_context(tc.manual_schedule())
+
+        ident = keep.tile([P, P], F32, name="ident")
+        x_raw = [keep.tile([P, 2, K], U8, name="x_raw%d" % q) for q in range(NQ)]
+        x_sc = keep.tile([P, NT, 8], F32, name="x_sc")
+        c_raw = [keep.tile([P, 4, K], BF16, name="c_raw%d" % g) for g in range(NG)]
+        amp_sb = keep.tile([P, NG, 4], BF16, name="amp_sb")
+        row_bf = keep.tile([P, NT], BF16, name="row_bf")
+        row_sb = keep.tile([P, NT], F32, name="row_sb")
+        w_sb = keep.tile([P, NG, 2 * D], U8, name="w_sb", align_bytes=64)
+        w_sc = keep.tile([P, NG, D], U8, name="w_sc", align_bytes=64)
+        x_codes = [keep.tile([P, 2, QT], U32, name="x_codes%d" % q, align_bytes=64) for q in range(NQ)]
+        x_planes = [keep.tile([P, 2, QT], U8, name="x_planes%d" % q, align_bytes=64) for q in range(NQ)]
+        c_codes = [keep.tile([P, 2, P], U32, name="c_codes%d" % c, align_bytes=64) for c in range(4 * NG)]
+        c_planes = [keep.tile([P, 2, P], U8, name="c_planes%d" % c, align_bytes=64) for c in range(4 * NG)]
+        h_codes = [[keep.tile([P, QT], U32, name="h_codes%d_%d" % (q, g), align_bytes=64) for g in range(NG)] for q in range(NQ)]
+        h_planes = [[keep.tile([P, QT], U8, name="h_planes%d_%d" % (q, g), align_bytes=64) for g in range(NG)] for q in range(NQ)]
+
+        make_identity(nc, ident[:])
+
+        x_view = X_bytes.rearrange("(p i) k -> p i k", i=NT)
+        c_view = C.rearrange("(g m t) k -> g m t k", g=NG, t=4)
+        nc.sync.dma_start(out=c_raw[0][:, 0:1, :], in_=c_view[0][:, 0:1, :])
+        nc.sync.dma_start(out=x_sc[:], in_=X_scale.rearrange("(p i) b -> p i b", i=NT))
+        nc.sync.dma_start(out=x_raw[0][:], in_=x_view[:, 0:2, :])
+        for t in range(1, 4):
+            nc.sync.dma_start(out=c_raw[0][:, t : t + 1, :], in_=c_view[0][:, t : t + 1, :])
+        nc.sync.dma_start(out=amp_sb[:], in_=amp.rearrange("(g m t) -> m g t", g=NG, t=4))
+        for g in range(1, NG):
+            for t in (0, 2):
+                nc.sync.dma_start(out=c_raw[g][:, t : t + 2, :], in_=c_view[g][:, t : t + 2, :])
+            if g == 1:
+                nc.sync.dma_start(out=x_raw[1][:], in_=x_view[:, 2:4, :])
+        nc.gpsimd.memset(w_sc[:].rearrange("p g n -> p (g n)").bitcast(I32), 0)
+        for r in range(4):
+            nc.sync.dma_start(
+                out=w_sc[32 * r : 32 * r + 4, :, :].bitcast(I32),
+                in_=W_scales[:, 4 * r : 4 * r + 4, :].rearrange("g r n -> r g n").bitcast(I32),
+            )
+        for g in (0, 2):
+            nc.sync.dma_start(
+                out=w_sb[:, g : g + 2, :].bitcast(I32),
+                in_=W_words[g : g + 2].rearrange("g p w -> p g w").bitcast(I32),
+            )
+        nc.sync.dma_start(out=row_bf[:], in_=row.rearrange("(p i) -> p i", i=NT))
+        for q in (2, 3):
+            nc.sync.dma_start(out=x_raw[q][:], in_=x_view[:, 2 * q : 2 * q + 2, :])
+
+        warm = keep.tile([P, 1], F32, name="warm")
+        warm_out = keep.tile([P, 1], F32, name="warm_out")
+        nc.vector.memset(warm[:], 0.0)
+        nc.scalar.activation(out=warm_out[:], in_=warm[:], func=EXP)
+
+        x_bf, x_tr, x_grp, c_tr, c_grp = {}, {}, {}, {}, {}
+        z_bank, e_tile, h_grp, y_bank = {}, {}, {}, {}
+
+        def x_widen(q, i):
+            xb = stage.tile([P, K], BF16, tag="xb", name="xb")
+            x_bf[q, i] = xb
+            order = xb[:].rearrange("p (g u k e) -> p g k u e", g=2, u=2, e=2)
+            for b in range(8):
+                g, r = b // 4, b % 4
+                nc.vector.tensor_scalar(
+                    out=order[:, g, 32 * r : 32 * r + 32, :, :],
+                    in0=x_raw[q][:, i, P * b : P * b + P].bitcast(F8).rearrange("p (k u e) -> p k u e", u=2, e=2),
+                    scalar1=x_sc[:, 2 * q + i, b : b + 1],
+                    scalar2=None,
+                    op0=MULT,
+                )
+
+        def x_turn(q, i):
+            tr = psum.tile([P, 2, 2, P], F32, tag="bank", name="x_bank")
+            x_tr[q, i] = tr
+            words = x_bf.pop((q, i))[:].bitcast(F32)
+            for g in range(2):
+                for u in range(2):
+                    w0 = 256 * g + 128 * u
+                    nc.tensor.transpose(tr[:, g, u, :], words[:, w0 : w0 + P], ident[:])
+
+        def x_out(q, i, engine):
+            if i == 0:
+                x_grp[q] = stage.tile([P, 2, QT, 4], BF16, tag="x_grp", name="x_grp_t", align_bytes=64)
+            dst = x_grp[q][:, :, P * i : P * i + P, :].bitcast(F32)
+            src = x_tr.pop((q, i))[:].rearrange("p g u m -> p g m u")
+            if engine == "vector":
+                nc.vector.tensor_copy(out=dst, in_=src)
+            else:
+                nc.scalar.copy(out=dst, in_=src)
+
+        def x_quant(q):
+            grp = x_grp.pop(q)
+            for g in range(2):
+                nc.vector.quantize_mx(
+                    out=x_codes[q][:, g, :].bitcast(FP8X4),
+                    scales=x_planes[q][:, g, :],
+                    in_=grp[:, g, :, :].rearrange("p m j -> p (m j)"),
+                )
+
+        def c_turn(c):
+            tr = psum.tile([P, 2, 2, P], F32, tag="bank", name="c_bank")
+            c_tr[c] = tr
+            words = c_raw[c // 4][:, c % 4, :].bitcast(F32)
+            for g in range(2):
+                for u in range(2):
+                    nc.tensor.transpose(tr[:, g, u, :], words[:, 256 * g + u : 256 * (g + 1) : 2], ident[:])
+
+        def c_out(c):
+            grp = stage.tile([P, 2, P, 4], BF16, tag="c_grp", name="c_grp_t", align_bytes=64, bufs=4)
+            c_grp[c] = grp
+            nc.scalar.copy(out=grp[:].bitcast(F32), in_=c_tr.pop(c)[:].rearrange("p g u m -> p g m u"))
+
+        def c_quant(c):
+            nc.vector.quantize_mx(
+                out=c_codes[c][:].rearrange("p g m -> p (g m)").bitcast(FP8X4),
+                scales=c_planes[c][:].rearrange("p g m -> p (g m)"),
+                in_=c_grp.pop(c)[:].rearrange("p g m j -> p (g m j)"),
+            )
+
+        def first_product(g, q):
+            for a in range(2):
+                z = psum.tile([P, 2, QT], F32, tag="bank", name="z_bank_t")
+                z_bank[g, q, a] = z
+                for b in range(2):
+                    c = 4 * g + 2 * a + b
+                    for h in range(2):
+                        nc.tensor.matmul_mx(
+                            out=z[:, b, :],
+                            lhsT=c_codes[c][:, h, :].bitcast(FP8X4),
+                            lhsT_scale=c_planes[c][:, h, :],
+                            rhs=x_codes[q][:, h, :].bitcast(FP8X4),
+                            rhs_scale=x_planes[q][:, h, :],
+                            start=(h == 0),
+                            stop=(h == 1),
+                        )
+
+        def exponentials(g, q):
+            e = stage.tile([P, 2, QT, 2], F32, tag="e", name="e_t")
+            e_tile[g, q] = e
+            for a in range(2):
+                nc.scalar.activation(out=e[:, a, :, :], in_=z_bank.pop((g, q, a))[:].rearrange("p b t -> p t b"), func=EXP)
+
+        def times_amp(g, q):
+            hg = stage.tile([P, QT, 4], BF16, tag="h_grp", name="h_grp_t", align_bytes=64)
+            h_grp[g, q] = hg
+            e = e_tile.pop((g, q))
+            for t0 in range(0, QT, P):
+                nc.vector.tensor_tensor(
+                    out=hg[:, t0 : t0 + P, :].rearrange("p t (a b) -> p t a b", b=2),
+                    in0=e[:, :, t0 : t0 + P, :].rearrange("p a t b -> p t a b"),
+                    in1=amp_sb[:, g, :].rearrange("p (a b) -> p a b", b=2).unsqueeze(1).to_broadcast([P, P, 2, 2]),
+                    op=MULT,
+                )
+
+        def h_quant(g, q):
+            hg = h_grp.pop((g, q))
+            for t0 in range(0, QT, P):
+                nc.vector.quantize_mx(
+                    out=h_codes[q][g][:, t0 : t0 + P].bitcast(FP8X4),
+                    scales=h_planes[q][g][:, t0 : t0 + P],
+                    in_=hg[:, t0 : t0 + P, :].rearrange("p t j -> p (t j)"),
+                )
+
+        def second_product(q, u, gs):
+            i, dh = u // 2, u % 2
+            if gs[0] == 0:
+                y_bank[q, u] = psum.tile([P, 512], F32, tag="bank", name="y_bank_t")
+            for g in gs:
+                nc.tensor.matmul_mx(
+                    out=y_bank[q, u][:],
+                    lhsT=h_codes[q][g][:, P * i : P * i + P].bitcast(FP8X4),
+                    lhsT_scale=h_planes[q][g][:, P * i : P * i + P],
+                    rhs=w_sb[:, g, 1024 * dh : 1024 * dh + 1024].bitcast(FP4X4),
+                    rhs_scale=w_sc[:, g, 512 * dh : 512 * dh + 512],
+                    start=(g == 0),
+                    stop=(g == NG - 1),
+                )
+
+        out_view = out.rearrange("(p i) d -> p i d", i=NT)
+
+        def store(q, u, engine):
+            i, dh = 2 * q + u // 2, u % 2
+            y = stage.tile([P, 512], F32, tag="y", name="y_t", bufs=4)
+            if engine == "vector":
+                nc.vector.tensor_scalar(out=y[:], in0=y_bank.pop((q, u))[:], scalar1=row_sb[:, i : i + 1], scalar2=None, op0=MULT)
+            else:
+                nc.scalar.activation(out=y[:], in_=y_bank.pop((q, u))[:], func=COPY, scale=row_sb[:, i : i + 1])
+            nc.sync.dma_start(out=out_view[:, i, 512 * dh : 512 * dh + 512], in_=y[:])
+
+        x_widen(0, 0)
+        x_widen(0, 1)
+        c_turn(0)
+        c_out(0)
+        c_turn(1)
+        c_out(1)
+        x_turn(0, 0)
+        x_out(0, 0, "scalar")
+        c_turn(2)
+        c_out(2)
+        x_turn(0, 1)
+        x_out(0, 1, "vector")
+        c_turn(3)
+        c_out(3)
+        c_quant(0)
+        x_quant(0)
+        for c in range(1, 4):
+            c_quant(c)
+
+        pending = None
+        for g in range(NG):
+            if g < NG - 1:
+                if g == 2:
+                    x_turn(1, 0)
+                    x_turn(1, 1)
+                    x_out(1, 0, "scalar")
+                    x_out(1, 1, "scalar")
+                for c in range(4 * g + 4, 4 * g + 8):
+                    c_turn(c)
+                    c_out(c)
+                    c_quant(c)
+                    if c == 13:
+                        x_quant(1)
+                    if pending is not None and c == 4 * g + 4:
+                        h_quant(*pending)
+                        pending = None
+                if g < 2:
+                    x_widen(1, g)
+            else:
+                h_quant(*pending)
+            first_product(g, 0)
+            exponentials(g, 0)
+            times_amp(g, 0)
+            pending = (g, 0)
+
+        nc.vector.tensor_copy(out=row_sb[:], in_=row_bf[:])
+
+        units = []
+        done = None
+        for q in range(1, NQ):
+            for g in range(NG):
+                first_product(g, q)
+                h_quant(*pending)
+                exponentials(g, q)
+                if q + 1 < NQ and g < 2:
+                    x_widen(q + 1, g)
+                if q + 1 < NQ and g == 3:
+                    x_quant(q + 1)
+                times_amp(g, q)
+                pending = (g, q)
+                if q + 1 < NQ and g == 2:
+                    x_turn(q + 1, 0)
+                    x_turn(q + 1, 1)
+                if units:
+                    unit = units.pop(0)
+                    second_product(*unit, range(NG))
+                    if done is not None:
+                        store(*done, "scalar")
+                    done = unit
+                if q + 1 < NQ and g == 2:
+                    x_out(q + 1, 0, "scalar")
+                    x_out(q + 1, 1, "scalar")
+                if g == 0:
+                    units += [(q - 1, u) for u in range(4)]
+
+        h_quant(*pending)
+        unit = units.pop(0)
+        second_product(*unit, range(NG))
+        store(*done, "scalar")
+        store(*unit, "vector")
+        last = NQ - 1
+        for u in (0, 1):
+            second_product(last, u, range(NG - 1))
+        for u in (0, 1):
+            second_product(last, u, [NG - 1])
+            store(last, u, "scalar" if u % 2 == 0 else "vector")
+        second_product(last, 2, range(NG))
+        store(last, 2, "scalar")
+        second_product(last, 3, range(NG))
+        i = NT - 1
+        y = stage.tile([P, 512], F32, tag="y", name="y_t", bufs=4)
+        y2 = stage.tile([P, 256], F32, tag="y2", name="y2_t", bufs=1)
+        bank = y_bank.pop((last, 3))
+        nc.scalar.activation(out=y[:, 0:256], in_=bank[:, 0:256], func=COPY, scale=row_sb[:, i : i + 1])
+        nc.vector.tensor_scalar(out=y2[:], in0=bank[:, 256:512], scalar1=row_sb[:, i : i + 1], scalar2=None, op0=MULT)
+        nc.sync.dma_start(out=out_view[:, i, 512:768], in_=y[:, 0:256])
+        nc.sync.dma_start(out=out_view[:, i, 768:1024], in_=y2[:])

@@ -79,10 +79,17 @@ def tile_rbf_kernel_readout_d4_kernel(tc, X_bytes, X_scale, C, amp, row, W_words
         for q in (2, 3):
             nc.sync.dma_start(out=x_raw[q][:], in_=x_view[:, 2 * q : 2 * q + 2, :])
 
-        warm = keep.tile([P, 1], F32, name="warm")
+        warm = keep.tile([P, 512], BF16, name="warm")
         warm_out = keep.tile([P, 1], F32, name="warm_out")
         nc.vector.memset(warm[:], 0.0)
-        nc.scalar.activation(out=warm_out[:], in_=warm[:], func=EXP)
+        nc.scalar.activation(out=warm_out[:], in_=warm[:, 0:1], func=EXP)
+        warm_bank = psum.tile([P, 512], F32, tag="bank", name="warm_bank")
+
+        def spin(n):
+            for k in range(n):
+                nc.tensor.matmul(warm_bank[:], lhsT=warm[:, 0:P], rhs=warm[:], start=True, stop=True)
+
+        spin(4)
 
         x_bf, x_tr, x_grp, c_tr, c_grp = {}, {}, {}, {}, {}
         z_bank, e_tile, h_grp, y_bank = {}, {}, {}, {}
@@ -223,8 +230,10 @@ def tile_rbf_kernel_readout_d4_kernel(tc, X_bytes, X_scale, C, amp, row, W_words
         x_widen(0, 1)
         c_turn(0)
         c_out(0)
+        spin(2)
         c_turn(1)
         c_out(1)
+        spin(1)
         x_turn(0, 0)
         x_out(0, 0, "scalar")
         c_turn(2)
@@ -233,6 +242,7 @@ def tile_rbf_kernel_readout_d4_kernel(tc, X_bytes, X_scale, C, amp, row, W_words
         x_out(0, 1, "vector")
         c_turn(3)
         c_out(3)
+        spin(1)
         c_quant(0)
         x_quant(0)
         for c in range(1, 4):
@@ -250,6 +260,8 @@ def tile_rbf_kernel_readout_d4_kernel(tc, X_bytes, X_scale, C, amp, row, W_words
                     c_turn(c)
                     c_out(c)
                     c_quant(c)
+                    if c == 5:
+                        spin(1)
                     if c == 13:
                         x_quant(1)
                     if pending is not None and c == 4 * g + 4:

@@ -65,6 +65,8 @@ def tile_rbf_kernel_readout_d4_kernel(tc, X_bytes, X_scale, C, amp, row, W_words
             if g == 1:
                 nc.sync.dma_start(out=x_raw[1][:], in_=x_view[:, 2:4, :])
         nc.gpsimd.memset(w_sc[:].rearrange("p g n -> p (g n)").bitcast(I32), 0)
+        for q in (2, 3):
+            nc.sync.dma_start(out=x_raw[q][:], in_=x_view[:, 2 * q : 2 * q + 2, :])
         for r in range(4):
             nc.sync.dma_start(
                 out=w_sc[32 * r : 32 * r + 4, :, :].bitcast(I32),
@@ -76,8 +78,6 @@ def tile_rbf_kernel_readout_d4_kernel(tc, X_bytes, X_scale, C, amp, row, W_words
                 in_=W_words[g : g + 2].rearrange("g p w -> p g w").bitcast(I32),
             )
         nc.sync.dma_start(out=row_bf[:], in_=row.rearrange("(p i) -> p i", i=NT))
-        for q in (2, 3):
-            nc.sync.dma_start(out=x_raw[q][:], in_=x_view[:, 2 * q : 2 * q + 2, :])
 
         warm = keep.tile([P, 512], BF16, name="warm")
         warm_out = keep.tile([P, 1], F32, name="warm_out")
@@ -95,14 +95,12 @@ def tile_rbf_kernel_readout_d4_kernel(tc, X_bytes, X_scale, C, amp, row, W_words
         z_bank, e_tile, h_grp, y_bank = {}, {}, {}, {}
 
         def x_widen(q, i):
-            xb = stage.tile([P, K], BF16, tag="xb", name="xb")
+            xb = stage.tile([P, K], BF16, tag="xb", name="xb", bufs=4)
             x_bf[q, i] = xb
-            order = xb[:].rearrange("p (g u k e) -> p g k u e", g=2, u=2, e=2)
             for b in range(8):
-                g, r = b // 4, b % 4
                 nc.vector.tensor_scalar(
-                    out=order[:, g, 32 * r : 32 * r + 32, :, :],
-                    in0=x_raw[q][:, i, P * b : P * b + P].bitcast(F8).rearrange("p (k u e) -> p k u e", u=2, e=2),
+                    out=xb[:, P * b : P * b + P],
+                    in0=x_raw[q][:, i, P * b : P * b + P].bitcast(F8),
                     scalar1=x_sc[:, 2 * q + i, b : b + 1],
                     scalar2=None,
                     op0=MULT,
@@ -114,8 +112,7 @@ def tile_rbf_kernel_readout_d4_kernel(tc, X_bytes, X_scale, C, amp, row, W_words
             words = x_bf.pop((q, i))[:].bitcast(F32)
             for g in range(2):
                 for u in range(2):
-                    w0 = 256 * g + 128 * u
-                    nc.tensor.transpose(tr[:, g, u, :], words[:, w0 : w0 + P], ident[:])
+                    nc.tensor.transpose(tr[:, g, u, :], words[:, 256 * g + u : 256 * (g + 1) : 2], ident[:])
 
         def x_out(q, i, engine):
             if i == 0:
@@ -244,81 +241,93 @@ def tile_rbf_kernel_readout_d4_kernel(tc, X_bytes, X_scale, C, amp, row, W_words
         c_out(3)
         spin(1)
         c_quant(0)
+        c_quant(1)
         x_quant(0)
-        for c in range(1, 4):
+        c_quant(2)
+        c_quant(3)
+
+        for c in range(4, 8):
+            c_turn(c)
+            c_out(c)
             c_quant(c)
-
-        pending = None
-        for g in range(NG):
-            if g < NG - 1:
-                if g == 2:
-                    x_turn(1, 0)
-                    x_turn(1, 1)
-                    x_out(1, 0, "scalar")
-                    x_out(1, 1, "scalar")
-                for c in range(4 * g + 4, 4 * g + 8):
-                    c_turn(c)
-                    c_out(c)
-                    c_quant(c)
-                    if c == 5:
-                        spin(1)
-                    if c == 13:
-                        x_quant(1)
-                    if pending is not None and c == 4 * g + 4:
-                        h_quant(*pending)
-                        pending = None
-                if g < 2:
-                    x_widen(1, g)
-            else:
-                h_quant(*pending)
-            first_product(g, 0)
-            exponentials(g, 0)
-            times_amp(g, 0)
-            pending = (g, 0)
-
+            if c == 5:
+                spin(1)
+        first_product(0, 0)
+        exponentials(0, 0)
+        x_widen(1, 0)
+        x_widen(1, 1)
+        for c in range(8, 12):
+            c_turn(c)
+            c_out(c)
+            c_quant(c)
+            if c == 8:
+                times_amp(0, 0)
+            if c == 9:
+                h_quant(0, 0)
+        first_product(1, 0)
+        exponentials(1, 0)
+        x_turn(1, 0)
+        x_turn(1, 1)
+        spin(1)
+        x_out(1, 0, "scalar")
+        x_out(1, 1, "scalar")
+        for c in range(12, 16):
+            c_turn(c)
+            c_out(c)
+            c_quant(c)
+            if c == 12:
+                times_amp(1, 0)
+            if c == 12+1:
+                h_quant(1, 0)
+            if c == 14:
+                x_quant(1)
         nc.vector.tensor_copy(out=row_sb[:], in_=row_bf[:])
 
-        units = []
-        done = None
-        for q in range(1, NQ):
-            for g in range(NG):
+        beside = {2: [(2, 0), (2, 1)], 3: [(3, 0)], 4: [(3, 1)]}
+        finished, fresh = [], []
+        units = [(q, u) for q in range(1, NQ) for u in range(4)]
+        for s in range(2, NQ * NG + 1):
+            q, g = s // NG, s % NG
+            if s < NQ * NG:
                 first_product(g, q)
-                h_quant(*pending)
                 exponentials(g, q)
-                if q + 1 < NQ and g < 2:
-                    x_widen(q + 1, g)
-                if q + 1 < NQ and g == 3:
-                    x_quant(q + 1)
-                times_amp(g, q)
-                pending = (g, q)
-                if q + 1 < NQ and g == 2:
-                    x_turn(q + 1, 0)
-                    x_turn(q + 1, 1)
-                if units:
-                    unit = units.pop(0)
-                    second_product(*unit, range(NG))
-                    if done is not None:
-                        store(*done, "scalar")
-                    done = unit
-                if q + 1 < NQ and g == 2:
-                    x_out(q + 1, 0, "scalar")
-                    x_out(q + 1, 1, "scalar")
-                if g == 0:
-                    units += [(q - 1, u) for u in range(4)]
-
-        h_quant(*pending)
-        unit = units.pop(0)
-        second_product(*unit, range(NG))
-        store(*done, "scalar")
-        store(*unit, "vector")
+            if s == 6:
+                for n in (2, 3):
+                    for i in range(2):
+                        x_turn(n, i)
+                for n in (2, 3):
+                    for i in range(2):
+                        x_out(n, i, "scalar")
+            if s > 2:
+                times_amp((s - 1) % NG, (s - 1) // NG)
+                for n in beside.get(s - 1, []):
+                    x_widen(*n)
+                if s == 6:
+                    x_quant(2)
+                if s == 6 + 1:
+                    x_quant(3)
+                h_quant((s - 1) % NG, (s - 1) // NG)
+            g = {2: 0, 4: 1, 5: 2, 7: 3}.get(s)
+            if g is not None:
+                for u in range(4):
+                    second_product(0, u, [g])
+                if g == NG - 1:
+                    fresh = [(0, u) for u in range(4)]
+            elif s >= 9 and s < NQ * NG:
+                unit = units.pop(0)
+                second_product(*unit, range(NG))
+                fresh = [unit]
+            for unit in finished[:2]:
+                store(*unit, "scalar")
+            finished = finished[2:] + fresh
+            fresh = []
         last = NQ - 1
-        for u in (0, 1):
-            second_product(last, u, range(NG - 1))
-        for u in (0, 1):
-            second_product(last, u, [NG - 1])
-            store(last, u, "scalar" if u % 2 == 0 else "vector")
-        second_product(last, 2, range(NG))
-        store(last, 2, "scalar")
+        for unit in finished:
+            store(*unit, "scalar")
+        while len(units) > 1:
+            unit = units.pop(0)
+            second_product(*unit, range(NG))
+            store(*unit, "scalar" if unit[1] % 2 == 0 else "vector")
         second_product(last, 3, range(NG))
         i = NT - 1
         y = stage.tile([P, 512], F32, tag="y", name="y_t", bufs=4)

from contextlib import ExitStack

import concourse.mybir as mybir
from concourse.masks import make_identity

T, K, J, D = 1024, 1024, 2048, 1024
FLOPS = 2 * T * K * J + 2 * T * J * D

F32 = mybir.dt.float32
BF16 = mybir.dt.bfloat16
U32 = mybir.dt.uint32
I32 = mybir.dt.int32
U8 = mybir.dt.uint8
F8 = mybir.dt.float8_e4m3fn
FP8X4 = mybir.dt.float8_e4m3fn_x4
FP4X4 = mybir.dt.float4_e2m1fn_x4
MULT = mybir.AluOpType.mult
EXP = mybir.ActivationFunctionType.Exp
COPY = mybir.ActivationFunctionType.Copy

P = 128
NT = T // P
NQ = 4
QT = T // NQ
NG = J // 512


def tile_rbf_kernel_readout_d4_kernel(tc, X_bytes, X_scale, C, amp, row, W_words, W_scales, out):
    nc = tc.nc
    with ExitStack() as ctx:
        keep = ctx.enter_context(tc.tile_pool(name="keep", bufs=1))
        stage = ctx.enter_context(tc.tile_pool(name="stage", bufs=3))
        psum = ctx.enter_context(tc.psum_pool(name="psum", bufs=8))
        ctx.enter_context(tc.manual_schedule())

        ident = keep.tile([P, P], F32, name="ident")
        x_raw = [keep.tile([P, 2, K], U8, name="x_raw%d" % q) for q in range(NQ)]
        x_sc = keep.tile([P, NT, 8], F32, name="x_sc")
        c_raw = [keep.tile([P, 4, K], BF16, name="c_raw%d" % g) for g in range(NG)]
        amp_sb = keep.tile([P, NG, 4], BF16, name="amp_sb")
        row_bf = keep.tile([P, NT], BF16, name="row_bf")
        row_sb = keep.tile([P, NT], F32, name="row_sb")
        w_sb = keep.tile([P, NG, 2 * D], U8, name="w_sb", align_bytes=64)
        w_sc = keep.tile([P, NG, D], U8, name="w_sc", align_bytes=64)
        x_codes = [keep.tile([P, 2, QT], U32, name="x_codes%d" % q, align_bytes=64) for q in range(NQ)]
        x_planes = [keep.tile([P, 2, QT], U8, name="x_planes%d" % q, align_bytes=64) for q in range(NQ)]
        c_codes = [keep.tile([P, 2, P], U32, name="c_codes%d" % c, align_bytes=64) for c in range(4 * NG)]
        c_planes = [keep.tile([P, 2, P], U8, name="c_planes%d" % c, align_bytes=64) for c in range(4 * NG)]
        h_codes = [[keep.tile([P, QT], U32, name="h_codes%d_%d" % (q, g), align_bytes=64) for g in range(NG)] for q in range(NQ)]
        h_planes = [[keep.tile([P, QT], U8, name="h_planes%d_%d" % (q, g), align_bytes=64) for g in range(NG)] for q in range(NQ)]

        make_identity(nc, ident[:])

        x_view = X_bytes.rearrange("(p i) k -> p i k", i=NT)
        c_view = C.rearrange("(g m t) k -> g m t k", g=NG, t=4)
        nc.sync.dma_start(out=c_raw[0][:, 0:1, :], in_=c_view[0][:, 0:1, :])
        nc.sync.dma_start(out=x_sc[:], in_=X_scale.rearrange("(p i) b -> p i b", i=NT))
        nc.sync.dma_start(out=x_raw[0][:], in_=x_view[:, 0:2, :])
        for t in range(1, 4):
            nc.sync.dma_start(out=c_raw[0][:, t : t + 1, :], in_=c_view[0][:, t : t + 1, :])
        nc.sync.dma_start(out=amp_sb[:], in_=amp.rearrange("(g m t) -> m g t", g=NG, t=4))
        for g in range(1, NG):
            for t in (0, 2):
                nc.sync.dma_start(out=c_raw[g][:, t : t + 2, :], in_=c_view[g][:, t : t + 2, :])
            if g == 1:
                nc.sync.dma_start(out=x_raw[1][:], in_=x_view[:, 2:4, :])
        nc.gpsimd.memset(w_sc[:].rearrange("p g n -> p (g n)").bitcast(I32), 0)
        for q in (2, 3):
            nc.sync.dma_start(out=x_raw[q][:], in_=x_view[:, 2 * q : 2 * q + 2, :])
        for r in range(4):
            nc.sync.dma_start(
                out=w_sc[32 * r : 32 * r + 4, :, :].bitcast(I32),
                in_=W_scales[:, 4 * r : 4 * r + 4, :].rearrange("g r n -> r g n").bitcast(I32),
            )
        for g in (0, 2):
            nc.sync.dma_start(
                out=w_sb[:, g : g + 2, :].bitcast(I32),
                in_=W_words[g : g + 2].rearrange("g p w -> p g w").bitcast(I32),
            )
        nc.sync.dma_start(out=row_bf[:], in_=row.rearrange("(p i) -> p i", i=NT))

        warm = keep.tile([P, 512], BF16, name="warm")
        warm_out = keep.tile([P, 1], F32, name="warm_out")
        nc.vector.memset(warm[:], 0.0)
        nc.scalar.activation(out=warm_out[:], in_=warm[:, 0:1], func=EXP)
        warm_bank = psum.tile([P, 512], F32, tag="bank", name="warm_bank")

        def spin(n):
            for k in range(n):
                nc.tensor.matmul(warm_bank[:], lhsT=warm[:, 0:P], rhs=warm[:], start=True, stop=True)

        spin(4)

        x_bf, x_tr, x_grp, c_tr, c_grp = {}, {}, {}, {}, {}
        z_bank, e_tile, h_grp, y_bank = {}, {}, {}, {}

        def x_widen(q, i):
            xb = stage.tile([P, K], BF16, tag="xb", name="xb", bufs=4)
            x_bf[q, i] = xb
            for b in range(8):
                nc.vector.tensor_scalar(
                    out=xb[:, P * b : P * b + P],
                    in0=x_raw[q][:, i, P * b : P * b + P].bitcast(F8),
                    scalar1=x_sc[:, 2 * q + i, b : b + 1],
                    scalar2=None,
                    op0=MULT,
                )

        def x_turn(q, i):
            tr = psum.tile([P, 2, 2, P], F32, tag="bank", name="x_bank")
            x_tr[q, i] = tr
            words = x_bf.pop((q, i))[:].bitcast(F32)
            for g in range(2):
                for u in range(2):
                    nc.tensor.transpose(tr[:, g, u, :], words[:, 256 * g + u : 256 * (g + 1) : 2], ident[:])

        def x_out(q, i, engine):
            if i == 0:
                x_grp[q] = stage.tile([P, 2, QT, 4], BF16, tag="x_grp", name="x_grp_t", align_bytes=64)
            dst = x_grp[q][:, :, P * i : P * i + P, :].bitcast(F32)
            src = x_tr.pop((q, i))[:].rearrange("p g u m -> p g m u")
            if engine == "vector":
                nc.vector.tensor_copy(out=dst, in_=src)
            else:
                nc.scalar.copy(out=dst, in_=src)

        def x_quant(q):
            grp = x_grp.pop(q)
            for g in range(2):
                nc.vector.quantize_mx(
                    out=x_codes[q][:, g, :].bitcast(FP8X4),
                    scales=x_planes[q][:, g, :],
                    in_=grp[:, g, :, :].rearrange("p m j -> p (m j)"),
                )

        def c_turn(c):
            tr = psum.tile([P, 2, 2, P], F32, tag="bank", name="c_bank")
            c_tr[c] = tr
            words = c_raw[c // 4][:, c % 4, :].bitcast(F32)
            for g in range(2):
                for u in range(2):
                    nc.tensor.transpose(tr[:, g, u, :], words[:, 256 * g + u : 256 * (g + 1) : 2], ident[:])

        def c_out(c):
            grp = stage.tile([P, 2, P, 4], BF16, tag="c_grp", name="c_grp_t", align_bytes=64, bufs=4)
            c_grp[c] = grp
            nc.scalar.copy(out=grp[:].bitcast(F32), in_=c_tr.pop(c)[:].rearrange("p g u m -> p g m u"))

        def c_quant(c):
            nc.vector.quantize_mx(
                out=c_codes[c][:].rearrange("p g m -> p (g m)").bitcast(FP8X4),
                scales=c_planes[c][:].rearrange("p g m -> p (g m)"),
                in_=c_grp.pop(c)[:].rearrange("p g m j -> p (g m j)"),
            )

        def first_product(g, q):
            for a in range(2):
                z = psum.tile([P, 2, QT], F32, tag="bank", name="z_bank_t")
                z_bank[g, q, a] = z
                for b in range(2):
                    c = 4 * g + 2 * a + b
                    for h in range(2):
                        nc.tensor.matmul_mx(
                            out=z[:, b, :],
                            lhsT=c_codes[c][:, h, :].bitcast(FP8X4),
                            lhsT_scale=c_planes[c][:, h, :],
                            rhs=x_codes[q][:, h, :].bitcast(FP8X4),
                            rhs_scale=x_planes[q][:, h, :],
                            start=(h == 0),
                            stop=(h == 1),
                        )

        def exponentials(g, q):
            e = stage.tile([P, 2, QT, 2], F32, tag="e", name="e_t")
            e_tile[g, q] = e
            for a in range(2):
                nc.scalar.activation(out=e[:, a, :, :], in_=z_bank.pop((g, q, a))[:].rearrange("p b t -> p t b"), func=EXP)

        def times_amp(g, q):
            hg = stage.tile([P, QT, 4], BF16, tag="h_grp", name="h_grp_t", align_bytes=64)
            h_grp[g, q] = hg
            e = e_tile.pop((g, q))
            for t0 in range(0, QT, P):
                nc.vector.tensor_tensor(
                    out=hg[:, t0 : t0 + P, :].rearrange("p t (a b) -> p t a b", b=2),
                    in0=e[:, :, t0 : t0 + P, :].rearrange("p a t b -> p t a b"),
                    in1=amp_sb[:, g, :].rearrange("p (a b) -> p a b", b=2).unsqueeze(1).to_broadcast([P, P, 2, 2]),
                    op=MULT,
                )

        def h_quant(g, q):
            hg = h_grp.pop((g, q))
            for t0 in range(0, QT, P):
                nc.vector.quantize_mx(
                    out=h_codes[q][g][:, t0 : t0 + P].bitcast(FP8X4),
                    scales=h_planes[q][g][:, t0 : t0 + P],
                    in_=hg[:, t0 : t0 + P, :].rearrange("p t j -> p (t j)"),
                )

        def second_product(q, u, gs):
            i, dh = u // 2, u % 2
            if gs[0] == 0:
                y_bank[q, u] = psum.tile([P, 512], F32, tag="bank", name="y_bank_t")
            for g in gs:
                nc.tensor.matmul_mx(
                    out=y_bank[q, u][:],
                    lhsT=h_codes[q][g][:, P * i : P * i + P].bitcast(FP8X4),
                    lhsT_scale=h_planes[q][g][:, P * i : P * i + P],
                    rhs=w_sb[:, g, 1024 * dh : 1024 * dh + 1024].bitcast(FP4X4),
                    rhs_scale=w_sc[:, g, 512 * dh : 512 * dh + 512],
                    start=(g == 0),
                    stop=(g == NG - 1),
                )

        out_view = out.rearrange("(p i) d -> p i d", i=NT)

        def store(q, u, engine):
            i, dh = 2 * q + u // 2, u % 2
            y = stage.tile([P, 512], F32, tag="y", name="y_t", bufs=4)
            if engine == "vector":
                nc.vector.tensor_scalar(out=y[:], in0=y_bank.pop((q, u))[:], scalar1=row_sb[:, i : i + 1], scalar2=None, op0=MULT)
            else:
                nc.scalar.activation(out=y[:], in_=y_bank.pop((q, u))[:], func=COPY, scale=row_sb[:, i : i + 1])
            nc.sync.dma_start(out=out_view[:, i, 512 * dh : 512 * dh + 512], in_=y[:])

        x_widen(0, 0)
        x_widen(0, 1)
        c_turn(0)
        c_out(0)
        spin(2)
        c_turn(1)
        c_out(1)
        spin(1)
        x_turn(0, 0)
        x_out(0, 0, "scalar")
        c_turn(2)
        c_out(2)
        x_turn(0, 1)
        x_out(0, 1, "vector")
        c_turn(3)
        c_out(3)
        spin(1)
        c_quant(0)
        c_quant(1)
        x_quant(0)
        c_quant(2)
        c_quant(3)

        for c in range(4, 8):
            c_turn(c)
            c_out(c)
            c_quant(c)
            if c == 5:
                spin(1)
        first_product(0, 0)
        exponentials(0, 0)
        x_widen(1, 0)
        x_widen(1, 1)
        for c in range(8, 12):
            c_turn(c)
            c_out(c)
            c_quant(c)
            if c == 8:
                times_amp(0, 0)
            if c == 9:
                h_quant(0, 0)
        first_product(1, 0)
        exponentials(1, 0)
        x_turn(1, 0)
        x_turn(1, 1)
        spin(1)
        x_out(1, 0, "scalar")
        x_out(1, 1, "scalar")
        for c in range(12, 16):
            c_turn(c)
            c_out(c)
            c_quant(c)
            if c == 12:
                times_amp(1, 0)
            if c == 12+1:
                h_quant(1, 0)
            if c == 14:
                x_quant(1)
        nc.vector.tensor_copy(out=row_sb[:], in_=row_bf[:])

        beside = {2: [(2, 0), (2, 1)], 3: [(3, 0)], 4: [(3, 1)]}
        finished, fresh = [], []
        units = [(q, u) for q in range(1, NQ) for u in range(4)]
        for s in range(2, NQ * NG + 1):
            q, g = s // NG, s % NG
            if s < NQ * NG:
                first_product(g, q)
                exponentials(g, q)
            if s == 6:
                for n in (2, 3):
                    for i in range(2):
                        x_turn(n, i)
                for n in (2, 3):
                    for i in range(2):
                        x_out(n, i, "scalar")
            if s > 2:
                times_amp((s - 1) % NG, (s - 1) // NG)
                for n in beside.get(s - 1, []):
                    x_widen(*n)
                if s == 6:
                    x_quant(2)
                if s == 6 + 1:
                    x_quant(3)
                h_quant((s - 1) % NG, (s - 1) // NG)
            g = {2: 0, 4: 1, 5: 2, 7: 3}.get(s)
            if g is not None:
                for u in range(4):
                    second_product(0, u, [g])
                if g == NG - 1:
                    fresh = [(0, u) for u in range(4)]
            elif s >= 9 and s < NQ * NG:
                unit = units.pop(0)
                second_product(*unit, range(NG))
                fresh = [unit]
            for unit in finished[:2]:
                store(*unit, "scalar")
            finished = finished[2:] + fresh
            fresh = []
        last = NQ - 1
        for unit in finished:
            store(*unit, "scalar")
        while len(units) > 1:
            unit = units.pop(0)
            second_product(*unit, range(NG))
            store(*unit, "scalar" if unit[1] % 2 == 0 else "vector")
        second_product(last, 3, range(NG))
        i = NT - 1
        y = stage.tile([P, 512], F32, tag="y", name="y_t", bufs=4)
        y2 = stage.tile([P, 256], F32, tag="y2", name="y2_t", bufs=1)
        bank = y_bank.pop((last, 3))
        nc.scalar.activation(out=y[:, 0:256], in_=bank[:, 0:256], func=COPY, scale=row_sb[:, i : i + 1])
        nc.vector.tensor_scalar(out=y2[:], in0=bank[:, 256:512], scalar1=row_sb[:, i : i + 1], scalar2=None, op0=MULT)
        nc.sync.dma_start(out=out_view[:, i, 512:768], in_=y[:, 0:256])
        nc.sync.dma_start(out=out_view[:, i, 768:1024], in_=y2[:])
